import numpy as np
import ml_dtypes


def mxq(x, axis, fmt="e4m3"):
    dtype, down = {"e4m3": (ml_dtypes.float8_e4m3fn, 7), "e5m2": (ml_dtypes.float8_e5m2, 14)}[fmt]
    v = np.moveaxis(np.asarray(x, np.float32).astype(ml_dtypes.bfloat16).astype(np.float64), axis, -1)
    blocks = v.reshape(v.shape[:-1] + (-1, 32))
    amax = np.abs(blocks).max(-1, keepdims=True)
    byte = np.maximum(np.where(amax > 0, np.frexp(amax)[1] - 1 + 127, 0) - down, 1)
    scale = np.exp2(byte - 127.0)
    codes = (blocks / scale).astype(np.float32).astype(dtype).astype(np.float64)
    return np.moveaxis((codes * scale).reshape(v.shape), -1, axis)


WIDE = False


def mx_kscale(k):
    if not WIDE:
        return np.ones(k)
    levels = np.array([10, -10, 5, -5, 0])
    if k % 512:
        return np.exp2(np.random.permutation(np.resize(levels, k // 32))).repeat(32)
    a = np.empty((k // 512, 16))
    for p in range(k // 512):
        a[p, :8] = np.random.permutation(np.resize(levels, 8))
        for g in range(8):
            far = levels[np.abs(levels - a[p, g]) >= 10]
            a[p, g + 8] = far[np.random.randint(len(far))]
    return np.exp2(a.ravel()).repeat(32)


BF16 = ml_dtypes.bfloat16


def bf(x):
    return np.asarray(x, np.float32).astype(BF16)


def f64(x):
    return np.asarray(x).astype(np.float64)


E2M1 = np.array([0.0, 0.5, 1.0, 1.5, 2.0, 3.0, 4.0, 6.0, -0.0, -0.5, -1.0, -1.5, -2.0, -3.0, -4.0, -6.0])


def pack_weight(w, fmt):
    k, n = w.shape
    w = f64(bf(w)).reshape(k // 32, 32, n)
    amax = np.abs(w).max(1)
    if fmt == "e4m3":
        byte = np.frexp(amax)[1] - 1 + 127 - 7
    else:
        mant, ex = np.frexp(amax / 6.0)
        byte = np.where(mant > 0.5, ex, ex - 1) + 127
    byte = np.clip(np.where(amax > 0, byte, 1), 1, 254)
    scaled = (w * np.exp2(127.0 - byte)[:, None, :]).reshape(k, n).astype(np.float32)
    by_word = np.ascontiguousarray(scaled.reshape(k // 512, 128, 4, n).transpose(0, 1, 3, 2))
    if fmt == "e4m3":
        words = by_word.astype(ml_dtypes.float8_e4m3fn).view(np.uint8)
    else:
        c = by_word.astype(ml_dtypes.float4_e2m1fn).view(np.uint8) & 0xF
        words = c[..., 0::2] | (c[..., 1::2] << 4)
    return np.ascontiguousarray(words), np.ascontiguousarray(byte.astype(np.uint8).reshape(k // 512, 16, n))


def unpack_weight(words, scales, fmt):
    g, p, n, _ = words.shape
    if fmt == "e4m3":
        vals = np.ascontiguousarray(words).view(ml_dtypes.float8_e4m3fn).astype(np.float64)
    else:
        nib = np.empty((g, p, n, 4), np.uint8)
        nib[..., 0::2] = words & 0xF
        nib[..., 1::2] = words >> 4
        vals = E2M1[nib]
    vals = vals * np.repeat(np.exp2(scales.astype(np.float64) - 127.0), 8, axis=1)[..., None]
    return vals.transpose(0, 1, 3, 2).reshape(g * 512, n)
def pack4(w):
    words, scales = pack_weight(w, "e2m1")
    return words.reshape(words.shape[0], 128, -1), scales


def unpack4(words, scales):
    return unpack_weight(words.reshape(words.shape[0], 128, -1, 2), scales, "e2m1")


def planes(Y):
    n, m = Y.shape
    b = f64(bf(Y)).reshape(n // 32, 32, m)
    amax = np.abs(b).max(1)
    byte = np.clip(np.where(amax > 0, np.frexp(amax)[1] - 1 + 127 - 7, 1), 1, 254)
    codes = (b * np.exp2(127.0 - byte)[:, None, :]).reshape(n, m).astype(np.float32).astype(ml_dtypes.float8_e4m3fn).view(np.uint8)
    words = codes.reshape(n // 512, 128, 4, m).transpose(0, 1, 3, 2)
    return np.ascontiguousarray(words), np.ascontiguousarray(byte.astype(np.uint8).reshape(n // 512, 16, m))


N, T, M, R, K = 512, 1024, 1024, 512, 1024


def weighted_energy(t, w):
    return np.sum(w[None, :] * np.square(t), axis=1)


def setup_inputs():
    s, u = mx_kscale(M), mx_kscale(R)
    amp_a = np.random.uniform(0.5, 1.5, (N, 1))
    amp_x = np.random.uniform(0.5, 1.5, (T, 1))
    a = bf(np.random.standard_normal((N, M)) * amp_a * s[None, :])
    x = bf(np.random.standard_normal((T, M)) * amp_x * s[None, :])
    l_words, l_scales = pack4(np.random.standard_normal((M, R)) / np.sqrt(M) / s[:, None] * u[None, :])
    return {"a": a,
            "x": x,
            "l_words": l_words,
            "l_scales": l_scales,
            "w": bf(np.random.uniform(0.5, 1.5, (R,)) / (u * u))}


def core(a, x, l_words, l_scales, w):
    w = f64(w)
    lq = unpack4(l_words, l_scales)
    ta = mxq(f64(a), 1, "e4m3") @ lq
    tx = mxq(f64(x), 1, "e4m3") @ lq
    qa = weighted_energy(ta, w)
    qx = weighted_energy(tx, w)
    b = mxq(ta * w[None, :], 1, "e4m3") @ mxq(tx, 1, "e4m3").T
    return K * np.square(b) / (qa[:, None] * (K + qx[None, :]))


def reference(a, x, l_words, l_scales, w):
    R_out = core(a, x, l_words, l_scales, w)
    words, scales = planes(R_out.T)
    return R_out, words, scales

@@ -1,0 +1,269 @@
+from contextlib import ExitStack
+
+import concourse.mybir as mybir
+from concourse.masks import make_identity
+
+N, T, M, R = 512, 1024, 1024, 512
+K_CONST = 1024.0
+CAST_V = 2
+P = 128
+FLOPS = 2 * (N + T) * M * R + 2 * N * T * R
+
+F32 = mybir.dt.float32
+BF16 = mybir.dt.bfloat16
+U32 = mybir.dt.uint32
+I32 = mybir.dt.int32
+U8 = mybir.dt.uint8
+FP8X4 = mybir.dt.float8_e4m3fn_x4
+FP4X4 = mybir.dt.float4_e2m1fn_x4
+ALU = mybir.AluOpType
+ACT = mybir.ActivationFunctionType
+
+
+def tile_reducedrankkellyglrtmap_kernel(tc, a, x, l_words, l_scales, w, out_0, out_1, out_2):
+    nc = tc.nc
+    XT = T // P
+    AT = N // P
+    NT = XT + AT
+    with ExitStack() as ctx:
+        keep = ctx.enter_context(tc.tile_pool(name="keep", bufs=1))
+        raw = ctx.enter_context(tc.tile_pool(name="raw", bufs=NT))
+        work = ctx.enter_context(tc.tile_pool(name="work", bufs=3))
+        tps = ctx.enter_context(tc.psum_pool(name="tps", bufs=2))
+        acc = ctx.enter_context(tc.psum_pool(name="acc", bufs=4))
+        rxp = ctx.enter_context(tc.psum_pool(name="rxp", bufs=2))
+
+        rows = [x[P * i : P * i + P, :] for i in range(XT)] + [a[P * i : P * i + P, :] for i in range(AT)]
+        tiles = []
+        lw = keep.tile([P, 2, 1024], U8, align_bytes=64, name="lw")
+        scr = keep.tile([P, 2, 512], U8, align_bytes=64, name="scr")
+        nc.vector.memset(scr[:].rearrange("p g n -> p (g n)").bitcast(I32), 0)
+        wt = keep.tile([P, P], BF16, align_bytes=64, name="wt")
+        nc.vector.memset(wt[:], 0.0)
+        ident = keep.tile([P, P], F32, align_bytes=64, name="ident")
+        make_identity(nc, ident[:])
+        warm = keep.tile([P, 4], F32, name="warm")
+        nc.vector.memset(warm[:], 0.0)
+        for n in range(NT):
+            rt = raw.tile([P, M], BF16, align_bytes=64, name="rt")
+            if n == 0:
+                for h in range(2):
+                    nc.sync.dma_start(out=rt[:, 512 * h : 512 * h + 512], in_=rows[n][:, 512 * h : 512 * h + 512])
+            else:
+                nc.sync.dma_start(out=rt[:], in_=rows[n])
+            tiles.append(rt)
+            if n == 0:
+                nc.sync.dma_start(out=lw[:].bitcast(I32), in_=l_words.bitcast(I32).rearrange("g p n -> p g n"))
+                for qd in range(4):
+                    nc.scalar.dma_start(
+                        out=scr[32 * qd : 32 * qd + 4, :, :].bitcast(I32),
+                        in_=l_scales[:, 4 * qd : 4 * qd + 4, :].bitcast(I32).rearrange("g q n -> q g n"),
+                    )
+                nc.scalar.dma_start(
+                    out=wt[0:4, :].rearrange("t (b i) -> t b i", i=8),
+                    in_=w.rearrange("(b t i) -> t b i", t=4, i=8),
+                )
+                nc.scalar.activation(out=warm[:], in_=warm[:], func=ACT.Square)
+
+        lp = keep.tile([P, 2, 4, 256], U8, align_bytes=64, name="lp")
+        sp = keep.tile([P, 2, 4, P], U8, align_bytes=64, name="sp")
+        def lprep():
+          for g in range(2):
+            nc.vector.tensor_copy(
+                out=lp[:, g, :, :].bitcast(I32).rearrange("p t (b i) -> p t b i", i=4),
+                in_=lw[:, g, :].bitcast(I32).rearrange("p (b t i) -> p t b i", t=4, i=4),
+            )
+            nc.vector.tensor_copy(
+                out=sp[:, g, :, :].bitcast(I32).rearrange("p t (b i) -> p t b i", i=2),
+                in_=scr[:, g, :].bitcast(I32).rearrange("p (b t i) -> p t b i", t=4, i=2),
+            )
+        wf = keep.tile([P, P], F32, name="wf")
+        wcol = keep.tile([P, 4], F32, name="wcol")
+
+        def wprep():
+            nc.vector.tensor_copy(out=wf[:], in_=wt[:])
+            wps = acc.tile([P, 512], F32, tag="acc", name="wps")
+            nc.tensor.transpose(wps[:, 0:P], wf[:], ident[:])
+            nc.vector.tensor_copy(out=wcol[:], in_=wps[:, 0:4])
+
+        x2c = keep.tile([P, T], U32, align_bytes=64, name="x2c")
+        x2s = keep.tile([P, T], U8, align_bytes=64, name="x2s")
+        a2c = keep.tile([P, N], U32, align_bytes=64, name="a2c")
+        a2s = keep.tile([P, N], U8, align_bytes=64, name="a2s")
+        psc = keep.tile([P, 2, N], U8, align_bytes=64, name="psc")
+        st = {}
+
+        def tin(n):
+            words = tiles[n][:].bitcast(F32)
+            tp = tps.tile([P, 4, P], F32, tag="tp", name="tp")
+            for g in range(2):
+                for u in range(2):
+                    nc.tensor.transpose(tp[:, 2 * g + u, :], words[:, 256 * g + u : 256 * (g + 1) : 2], ident[:])
+            st["tp", n] = tp
+
+        def copy(n):
+            xg = work.tile([P, 2, P, 4], BF16, align_bytes=64, tag="xg", name="xg")
+            nc.scalar.copy(out=xg[:].bitcast(F32), in_=st["tp", n][:].rearrange("p (g u) r -> p g r u", g=2))
+            st["xg", n] = xg
+
+        def quant(n):
+            xc = work.tile([P, 2 * P], U32, align_bytes=64, tag="xc", name="xc")
+            xs = work.tile([P, 2 * P], U8, align_bytes=64, tag="xs", name="xs")
+            nc.vector.quantize_mx(out=xc[:].bitcast(FP8X4), scales=xs[:], in_=st["xg", n][:].rearrange("p g r e -> p (g r e)"))
+            st["xc", n] = xc
+            st["xs", n] = xs
+
+        def s1(n):
+            ps = acc.tile([P, 4, P], F32, tag="acc", name="ps")
+            for t in range(4):
+                for g in range(2):
+                    c = slice(P * g, P * g + P)
+                    nc.tensor.matmul_mx(
+                        out=ps[:, t, :],
+                        lhsT=lp[:, g, t, :].bitcast(FP4X4),
+                        lhsT_scale=sp[:, g, t, :],
+                        rhs=st["xc", n][:, c].bitcast(FP8X4),
+                        rhs_scale=st["xs", n][:, c],
+                        start=(g == 0),
+                        stop=(g == 1),
+                    )
+            st["ps", n] = ps
+
+        def inter(n):
+            xb = work.tile([P, P, 4], BF16, align_bytes=64, tag="xb", name="xb")
+            src = st["ps", n][:].rearrange("p t n -> p n t")
+            if n < XT:
+                nc.vector.tensor_copy(out=xb[:], in_=src)
+            else:
+                nc.vector.tensor_tensor(out=xb[:], in0=src, in1=wcol[:].unsqueeze(1).to_broadcast([P, P, 4]), op=ALU.mult)
+            st["xb", n] = xb
+
+        def square(n):
+            sq = work.tile([P, 4, P], F32, tag="sq", name="sq")
+            nc.scalar.activation(out=sq[:], in_=st["ps", n][:], func=ACT.Square)
+            st["sq", n] = sq
+
+        def quant2(n):
+            m = n if n < XT else n - XT
+            codes, scales = (x2c, x2s) if n < XT else (a2c, a2s)
+            c = slice(P * m, P * m + P)
+            nc.vector.quantize_mx(out=codes[:, c].bitcast(FP8X4), scales=scales[:, c], in_=st["xb", n][:].rearrange("p n t -> p (n t)"))
+
+        def qsum(n):
+            m = n % 4 if n < XT else 0
+            if m == 0:
+                st["q"] = acc.tile([P, 512], F32, tag="acc", name="qps")
+            q = st["q"]
+            for t in range(4):
+                nc.tensor.matmul(q[:, m : m + 1], st["sq", n][:, t, :], wcol[:, t : t + 1], start=(t == 0), stop=(t == 3))
+
+        def norm(n):
+            q = st["q"]
+            if n < XT and n % 4 == 3:
+                den = work.tile([P, 4], F32, tag="den", name="den")
+                nc.vector.tensor_scalar(out=den[:], in0=q[:, 0:4], scalar1=1.0 / K_CONST, scalar2=1.0, op0=ALU.mult, op1=ALU.add)
+                rec = work.tile([P, 4], F32, tag="rec", name="rec")
+                nc.vector.reciprocal(out=rec[:], in_=den[:])
+                st["rec", n] = rec
+            if n >= XT:
+                ra = work.tile([P, 1], F32, tag="ra", name="ra")
+                nc.vector.reciprocal(out=ra[:], in_=q[:, 0:1])
+                st["ra", n - XT] = ra
+
+        def spread(n):
+            if n < XT and n % 4 == 3:
+                rec = st["rec", n]
+                rx = rxp.tile([P, 512], F32, tag="rx", name="rx")
+                for k in range(4):
+                    nc.tensor.transpose(rx[:, P * k : P * k + P], rec[:, k : k + 1].to_broadcast([P, P]), ident[:])
+                st["rx", n // 4] = rx
+
+        def prod(i, jg):
+            c = slice(512 * jg, 512 * jg + 512)
+            bp = acc.tile([P, 512], F32, tag="acc", name="bp")
+            nc.tensor.matmul_mx(
+                out=bp[:],
+                lhsT=a2c[:, P * i : P * i + P].bitcast(FP8X4),
+                lhsT_scale=a2s[:, P * i : P * i + P],
+                rhs=x2c[:, c].bitcast(FP8X4),
+                rhs_scale=x2s[:, c],
+                start=True,
+                stop=True,
+            )
+            st["bp", i, jg] = bp
+
+        def bsq(i, jg):
+            sb = work.tile([P, 512], F32, tag="sb", name="sb")
+            nc.scalar.activation(out=sb[:], in_=st["bp", i, jg][:], func=ACT.Square)
+            st["sb", i, jg] = sb
+
+        def form(i, jg):
+            c = slice(512 * jg, 512 * jg + 512)
+            if jg == 0:
+                st["y", i] = work.tile([P, T], F32, tag="y", name="y")
+            y = st["y", i]
+            nc.vector.scalar_tensor_tensor(out=y[:, c], in0=st["sb", i, jg][:], scalar=st["ra", i][:], in1=st["rx", jg][:], op0=ALU.mult, op1=ALU.mult)
+            nc.sync.dma_start(out=out_0[P * i : P * i + P, c], in_=y[:, c])
+
+        def cast(i, jg):
+            c = slice(512 * jg, 512 * jg + 512)
+            if jg == 0:
+                st["yb", i] = work.tile([P, T], BF16, align_bytes=64, tag="yb", name="yb")
+            y, yb = st["y", i], st["yb", i]
+            if i < CAST_V:
+                nc.gpsimd.tensor_scalar(out=yb[:, c], in0=y[:, c], scalar1=1.0, scalar2=0.0, op0=ALU.mult, op1=ALU.add)
+            else:
+                nc.vector.tensor_copy(out=yb[:, c], in_=y[:, c])
+
+        words_out = out_1.bitcast(I32).rearrange("g p m o -> p g (m o)")
+        scales_out = out_2.bitcast(I32)
+
+        def tout(i, jg):
+            words = st["yb", i][:].bitcast(F32)
+            if jg == 0:
+                st["to", i] = tps.tile([P, 4, P], F32, tag="tp", name="to")
+            for u in range(2):
+                nc.tensor.transpose(st["to", i][:, 2 * jg + u, :], words[:, 256 * jg + u : 256 * (jg + 1) : 2], ident[:])
+
+        def pcopy(i, jg):
+            if jg == 0:
+                st["pg", i] = work.tile([P, 2, P, 4], BF16, align_bytes=64, tag="pg", name="pg")
+            nc.scalar.copy(out=st["pg", i][:, jg, :, :].bitcast(F32), in_=st["to", i][:, 2 * jg : 2 * jg + 2, :].rearrange("p u r -> p r u"))
+
+        def pquant(i, jg):
+            if jg == 0:
+                st["pc", i] = work.tile([P, 2, P], U32, align_bytes=64, tag="pc", name="pc")
+            pc = st["pc", i]
+            nc.vector.quantize_mx(
+                out=pc[:, jg, :].bitcast(FP8X4),
+                scales=psc[:, jg, P * i : P * i + P],
+                in_=st["pg", i][:, jg, :, :].rearrange("p r e -> p (r e)"),
+            )
+            if jg == 1:
+                nc.sync.dma_start(out=words_out[:, :, P * i : P * i + P], in_=pc[:].bitcast(I32))
+            if i == AT - 1 and jg == 1:
+                for qd in range(4):
+                    nc.sync.dma_start(
+                        out=scales_out[:, 4 * qd : 4 * qd + 4, :].rearrange("g q n -> q g n"),
+                        in_=psc[32 * qd : 32 * qd + 4, :, :].bitcast(I32),
+                    )
+
+        plan = [
+            (prod, 3, 0), (bsq, 3, 0), (prod, 3, 1), (bsq, 3, 1),
+            (tin, 0, None), (copy, 0, None), (quant2, 2, None), (s1, 1, None), (square, 1, None), (qsum, 2, None), (quant, 0, None),
+            (norm, 2, None), (inter, 1, None), (spread, 3, None),
+            (form, 3, 0), (form, 3, 1), (cast, 3, 0), (cast, 3, 1),
+            (tout, 5, 0), (tout, 5, 1), (pcopy, 5, 0), (pcopy, 5, 1), (pquant, 5, 0), (pquant, 5, 1),
+        ]
+        ctx.enter_context(tc.manual_schedule())
+        for s in range(NT + 12):
+            for fn, lag, half in plan:
+                n = s - lag
+                if half is None and 0 <= n < NT:
+                    fn(n)
+                if half is not None and XT <= n < NT:
+                    fn(n - XT, half)
+            if s == 0:
+                lprep()
+            if s == 1:
+                wprep()

@@ -5,6 +5,7 @@ from concourse.masks import make_identity
 
 N, T, M, R = 512, 1024, 1024, 512
 K_CONST = 1024.0
+PER = [0,4,4,4,4,3,3,3,2,2,2,2]
 CAST_V = 2
 P = 128
 FLOPS = 2 * (N + T) * M * R + 2 * N * T * R
@@ -35,6 +36,11 @@ def tile_reducedrankkellyglrtmap_kernel(tc, a, x, l_words, l_scales, w, out_0, o
 
         rows = [x[P * i : P * i + P, :] for i in range(XT)] + [a[P * i : P * i + P, :] for i in range(AT)]
         tiles = []
+        zb = keep.tile([P, 512], BF16, align_bytes=64, name="zb")
+        nc.vector.memset(zb[:], 0.0)
+        wm = acc.tile([P, 512], F32, tag="acc", name="wm")
+        for k in range(4):
+            nc.tensor.matmul(wm[:], zb[:, 0:P], zb[:], start=True, stop=True)
         lw = keep.tile([P, 2, 1024], U8, align_bytes=64, name="lw")
         scr = keep.tile([P, 2, 512], U8, align_bytes=64, name="scr")
         nc.vector.memset(scr[:].rearrange("p g n -> p (g n)").bitcast(I32), 0)
@@ -44,6 +50,7 @@ def tile_reducedrankkellyglrtmap_kernel(tc, a, x, l_words, l_scales, w, out_0, o
         make_identity(nc, ident[:])
         warm = keep.tile([P, 4], F32, name="warm")
         nc.vector.memset(warm[:], 0.0)
+        nc.scalar.activation(out=warm[:], in_=warm[:], func=ACT.Square)
         for n in range(NT):
             rt = raw.tile([P, M], BF16, align_bytes=64, name="rt")
             if n == 0:
@@ -53,17 +60,16 @@ def tile_reducedrankkellyglrtmap_kernel(tc, a, x, l_words, l_scales, w, out_0, o
                 nc.sync.dma_start(out=rt[:], in_=rows[n])
             tiles.append(rt)
             if n == 0:
-                nc.sync.dma_start(out=lw[:].bitcast(I32), in_=l_words.bitcast(I32).rearrange("g p n -> p g n"))
                 for qd in range(4):
-                    nc.scalar.dma_start(
+                    nc.sync.dma_start(
                         out=scr[32 * qd : 32 * qd + 4, :, :].bitcast(I32),
                         in_=l_scales[:, 4 * qd : 4 * qd + 4, :].bitcast(I32).rearrange("g q n -> q g n"),
                     )
-                nc.scalar.dma_start(
+                nc.sync.dma_start(out=lw[:].bitcast(I32), in_=l_words.bitcast(I32).rearrange("g p n -> p g n"))
+                nc.sync.dma_start(
                     out=wt[0:4, :].rearrange("t (b i) -> t b i", i=8),
                     in_=w.rearrange("(b t i) -> t b i", t=4, i=8),
                 )
-                nc.scalar.activation(out=warm[:], in_=warm[:], func=ACT.Square)
 
         lp = keep.tile([P, 2, 4, 256], U8, align_bytes=64, name="lp")
         sp = keep.tile([P, 2, 4, P], U8, align_bytes=64, name="sp")
@@ -96,6 +102,8 @@ def tile_reducedrankkellyglrtmap_kernel(tc, a, x, l_words, l_scales, w, out_0, o
         def tin(n):
             words = tiles[n][:].bitcast(F32)
             tp = tps.tile([P, 4, P], F32, tag="tp", name="tp")
+            for k in range(PER[n]):
+                nc.tensor.matmul(tp[:, k % 4, :], zb[:, 0:P], zb[:, 0:P], start=True, stop=True)
             for g in range(2):
                 for u in range(2):
                     nc.tensor.transpose(tp[:, 2 * g + u, :], words[:, 256 * g + u : 256 * (g + 1) : 2], ident[:])

@@ -5,9 +5,9 @@ from concourse.masks import make_identity
 
 N, T, M, R = 512, 1024, 1024, 512
 K_CONST = 1024.0
-PER = [0,4,4,4,4,3,3,3,2,2,2,2]
-CAST_V = 2
 P = 128
+GROUP = 4
+QW = 64
 FLOPS = 2 * (N + T) * M * R + 2 * N * T * R
 
 F32 = mybir.dt.float32
@@ -23,34 +23,29 @@ ACT = mybir.ActivationFunctionType
 
 def tile_reducedrankkellyglrtmap_kernel(tc, a, x, l_words, l_scales, w, out_0, out_1, out_2):
     nc = tc.nc
-    XT = T // P
-    AT = N // P
-    NT = XT + AT
+    NT = (N + T) // P
     with ExitStack() as ctx:
         keep = ctx.enter_context(tc.tile_pool(name="keep", bufs=1))
         raw = ctx.enter_context(tc.tile_pool(name="raw", bufs=NT))
-        work = ctx.enter_context(tc.tile_pool(name="work", bufs=3))
-        tps = ctx.enter_context(tc.psum_pool(name="tps", bufs=2))
-        acc = ctx.enter_context(tc.psum_pool(name="acc", bufs=4))
-        rxp = ctx.enter_context(tc.psum_pool(name="rxp", bufs=2))
+        work = ctx.enter_context(tc.tile_pool(name="work", bufs=5))
+        psum = ctx.enter_context(tc.psum_pool(name="psum", bufs=8))
 
-        rows = [x[P * i : P * i + P, :] for i in range(XT)] + [a[P * i : P * i + P, :] for i in range(AT)]
-        tiles = []
-        zb = keep.tile([P, 512], BF16, align_bytes=64, name="zb")
-        nc.vector.memset(zb[:], 0.0)
-        wm = acc.tile([P, 512], F32, tag="acc", name="wm")
-        for k in range(4):
-            nc.tensor.matmul(wm[:], zb[:, 0:P], zb[:], start=True, stop=True)
-        lw = keep.tile([P, 2, 1024], U8, align_bytes=64, name="lw")
+        def bank(name):
+            return psum.tile([P, 512], F32, tag="bank", name=name)
+
         scr = keep.tile([P, 2, 512], U8, align_bytes=64, name="scr")
         nc.vector.memset(scr[:].rearrange("p g n -> p (g n)").bitcast(I32), 0)
         wt = keep.tile([P, P], BF16, align_bytes=64, name="wt")
         nc.vector.memset(wt[:], 0.0)
-        ident = keep.tile([P, P], F32, align_bytes=64, name="ident")
-        make_identity(nc, ident[:])
         warm = keep.tile([P, 4], F32, name="warm")
         nc.vector.memset(warm[:], 0.0)
         nc.scalar.activation(out=warm[:], in_=warm[:], func=ACT.Square)
+        ident = keep.tile([P, P], F32, align_bytes=64, name="ident")
+        make_identity(nc, ident[:])
+
+        rows = [a[P * i : P * i + P, :] for i in range(N // P)] + [x[P * i : P * i + P, :] for i in range(T // P)]
+        lw = keep.tile([P, 2, 1024], U8, align_bytes=64, name="lw")
+        tiles = []
         for n in range(NT):
             rt = raw.tile([P, M], BF16, align_bytes=64, name="rt")
             if n == 0:
@@ -61,57 +56,61 @@ def tile_reducedrankkellyglrtmap_kernel(tc, a, x, l_words, l_scales, w, out_0, o
             tiles.append(rt)
             if n == 0:
                 for qd in range(4):
-                    nc.sync.dma_start(
+                    nc.scalar.dma_start(
                         out=scr[32 * qd : 32 * qd + 4, :, :].bitcast(I32),
                         in_=l_scales[:, 4 * qd : 4 * qd + 4, :].bitcast(I32).rearrange("g q n -> q g n"),
                     )
-                nc.sync.dma_start(out=lw[:].bitcast(I32), in_=l_words.bitcast(I32).rearrange("g p n -> p g n"))
-                nc.sync.dma_start(
+                nc.scalar.dma_start(
                     out=wt[0:4, :].rearrange("t (b i) -> t b i", i=8),
                     in_=w.rearrange("(b t i) -> t b i", t=4, i=8),
                 )
+            if n == 1:
+                nc.sync.dma_start(out=lw[:].bitcast(I32), in_=l_words.bitcast(I32).rearrange("g p n -> p g n"))
 
         lp = keep.tile([P, 2, 4, 256], U8, align_bytes=64, name="lp")
         sp = keep.tile([P, 2, 4, P], U8, align_bytes=64, name="sp")
-        def lprep():
-          for g in range(2):
-            nc.vector.tensor_copy(
-                out=lp[:, g, :, :].bitcast(I32).rearrange("p t (b i) -> p t b i", i=4),
-                in_=lw[:, g, :].bitcast(I32).rearrange("p (b t i) -> p t b i", t=4, i=4),
-            )
-            nc.vector.tensor_copy(
-                out=sp[:, g, :, :].bitcast(I32).rearrange("p t (b i) -> p t b i", i=2),
-                in_=scr[:, g, :].bitcast(I32).rearrange("p (b t i) -> p t b i", t=4, i=2),
-            )
         wf = keep.tile([P, P], F32, name="wf")
         wcol = keep.tile([P, 4], F32, name="wcol")
+        wrep = keep.tile([P, 4, QW], F32, name="wrep")
+
+        def lprep():
+            for g in range(2):
+                nc.vector.tensor_copy(
+                    out=lp[:, g, :, :].bitcast(I32).rearrange("p t (b i) -> p t b i", i=4),
+                    in_=lw[:, g, :].bitcast(I32).rearrange("p (b t i) -> p t b i", t=4, i=4),
+                )
+            for g in range(2):
+                nc.vector.tensor_copy(
+                    out=sp[:, g, :, :].bitcast(I32).rearrange("p t (b i) -> p t b i", i=2),
+                    in_=scr[:, g, :].bitcast(I32).rearrange("p (b t i) -> p t b i", t=4, i=2),
+                )
 
         def wprep():
             nc.vector.tensor_copy(out=wf[:], in_=wt[:])
-            wps = acc.tile([P, 512], F32, tag="acc", name="wps")
+            wps = bank("wps")
             nc.tensor.transpose(wps[:, 0:P], wf[:], ident[:])
             nc.vector.tensor_copy(out=wcol[:], in_=wps[:, 0:4])
+            nc.vector.tensor_copy(out=wrep[:], in_=wcol[:].unsqueeze(2).to_broadcast([P, 4, QW]))
 
-        x2c = keep.tile([P, T], U32, align_bytes=64, name="x2c")
-        x2s = keep.tile([P, T], U8, align_bytes=64, name="x2s")
-        a2c = keep.tile([P, N], U32, align_bytes=64, name="a2c")
-        a2s = keep.tile([P, N], U8, align_bytes=64, name="a2s")
+        c2 = keep.tile([P, N + T], U32, align_bytes=64, name="c2")
+        s2 = keep.tile([P, N + T], U8, align_bytes=64, name="s2")
         psc = keep.tile([P, 2, N], U8, align_bytes=64, name="psc")
+        words_out = out_1.bitcast(I32).rearrange("g p m o -> p g (m o)")
+        scales_out = out_2.bitcast(I32)
         st = {}
 
         def tin(n):
             words = tiles[n][:].bitcast(F32)
-            tp = tps.tile([P, 4, P], F32, tag="tp", name="tp")
-            for k in range(PER[n]):
-                nc.tensor.matmul(tp[:, k % 4, :], zb[:, 0:P], zb[:, 0:P], start=True, stop=True)
+            tp = bank("tp")
             for g in range(2):
                 for u in range(2):
-                    nc.tensor.transpose(tp[:, 2 * g + u, :], words[:, 256 * g + u : 256 * (g + 1) : 2], ident[:])
+                    k = 2 * g + u
+                    nc.tensor.transpose(tp[:, P * k : P * k + P], words[:, 256 * g + u : 256 * (g + 1) : 2], ident[:])
             st["tp", n] = tp
 
         def copy(n):
             xg = work.tile([P, 2, P, 4], BF16, align_bytes=64, tag="xg", name="xg")
-            nc.scalar.copy(out=xg[:].bitcast(F32), in_=st["tp", n][:].rearrange("p (g u) r -> p g r u", g=2))
+            nc.scalar.copy(out=xg[:].bitcast(F32), in_=st["tp", n][:].rearrange("p (g u r) -> p g r u", g=2, u=2))
             st["xg", n] = xg
 
         def quant(n):
@@ -122,12 +121,12 @@ def tile_reducedrankkellyglrtmap_kernel(tc, a, x, l_words, l_scales, w, out_0, o
             st["xs", n] = xs
 
         def s1(n):
-            ps = acc.tile([P, 4, P], F32, tag="acc", name="ps")
+            ps = bank("ps")
             for t in range(4):
                 for g in range(2):
                     c = slice(P * g, P * g + P)
                     nc.tensor.matmul_mx(
-                        out=ps[:, t, :],
+                        out=ps[:, P * t : P * t + P],
                         lhsT=lp[:, g, t, :].bitcast(FP4X4),
                         lhsT_scale=sp[:, g, t, :],
                         rhs=st["xc", n][:, c].bitcast(FP8X4),
@@ -137,141 +136,165 @@ def tile_reducedrankkellyglrtmap_kernel(tc, a, x, l_words, l_scales, w, out_0, o
                     )
             st["ps", n] = ps
 
+        def square(n):
+            sq = work.tile([P, 4, P], F32, tag="sq", name="sq")
+            nc.scalar.activation(out=sq[:], in_=st["ps", n][:].rearrange("p (t n) -> p t n", t=4), func=ACT.Square)
+            st["sq", n] = sq
+
         def inter(n):
             xb = work.tile([P, P, 4], BF16, align_bytes=64, tag="xb", name="xb")
-            src = st["ps", n][:].rearrange("p t n -> p n t")
-            if n < XT:
+            src = st["ps", n][:].rearrange("p (t n) -> p n t", t=4)
+            if n >= GROUP:
                 nc.vector.tensor_copy(out=xb[:], in_=src)
             else:
                 nc.vector.tensor_tensor(out=xb[:], in0=src, in1=wcol[:].unsqueeze(1).to_broadcast([P, P, 4]), op=ALU.mult)
             st["xb", n] = xb
 
-        def square(n):
-            sq = work.tile([P, 4, P], F32, tag="sq", name="sq")
-            nc.scalar.activation(out=sq[:], in_=st["ps", n][:], func=ACT.Square)
-            st["sq", n] = sq
-
         def quant2(n):
-            m = n if n < XT else n - XT
-            codes, scales = (x2c, x2s) if n < XT else (a2c, a2s)
-            c = slice(P * m, P * m + P)
-            nc.vector.quantize_mx(out=codes[:, c].bitcast(FP8X4), scales=scales[:, c], in_=st["xb", n][:].rearrange("p n t -> p (n t)"))
+            c = slice(P * n, P * n + P)
+            nc.vector.quantize_mx(out=c2[:, c].bitcast(FP8X4), scales=s2[:, c], in_=st["xb", n][:].rearrange("p n t -> p (n t)"))
 
         def qsum(n):
-            m = n % 4 if n < XT else 0
+            gi, m = divmod(n, GROUP)
             if m == 0:
-                st["q"] = acc.tile([P, 512], F32, tag="acc", name="qps")
-            q = st["q"]
+                st["q", gi] = bank("qs")
+            q = st["q", gi]
             for t in range(4):
-                nc.tensor.matmul(q[:, m : m + 1], st["sq", n][:, t, :], wcol[:, t : t + 1], start=(t == 0), stop=(t == 3))
+                nc.tensor.matmul(q[:, QW * m : QW * m + QW], st["sq", n][:, t, :], wrep[:, t, :], start=(t == 0), stop=(t == 3))
 
-        def norm(n):
-            q = st["q"]
-            if n < XT and n % 4 == 3:
-                den = work.tile([P, 4], F32, tag="den", name="den")
-                nc.vector.tensor_scalar(out=den[:], in0=q[:, 0:4], scalar1=1.0 / K_CONST, scalar2=1.0, op0=ALU.mult, op1=ALU.add)
-                rec = work.tile([P, 4], F32, tag="rec", name="rec")
-                nc.vector.reciprocal(out=rec[:], in_=den[:])
-                st["rec", n] = rec
-            if n >= XT:
-                ra = work.tile([P, 1], F32, tag="ra", name="ra")
-                nc.vector.reciprocal(out=ra[:], in_=q[:, 0:1])
-                st["ra", n - XT] = ra
-
-        def spread(n):
-            if n < XT and n % 4 == 3:
-                rec = st["rec", n]
-                rx = rxp.tile([P, 512], F32, tag="rx", name="rx")
-                for k in range(4):
-                    nc.tensor.transpose(rx[:, P * k : P * k + P], rec[:, k : k + 1].to_broadcast([P, P]), ident[:])
-                st["rx", n // 4] = rx
-
-        def prod(i, jg):
-            c = slice(512 * jg, 512 * jg + 512)
-            bp = acc.tile([P, 512], F32, tag="acc", name="bp")
-            nc.tensor.matmul_mx(
-                out=bp[:],
-                lhsT=a2c[:, P * i : P * i + P].bitcast(FP8X4),
-                lhsT_scale=a2s[:, P * i : P * i + P],
-                rhs=x2c[:, c].bitcast(FP8X4),
-                rhs_scale=x2s[:, c],
-                start=True,
-                stop=True,
-            )
-            st["bp", i, jg] = bp
-
-        def bsq(i, jg):
-            sb = work.tile([P, 512], F32, tag="sb", name="sb")
-            nc.scalar.activation(out=sb[:], in_=st["bp", i, jg][:], func=ACT.Square)
-            st["sb", i, jg] = sb
-
-        def form(i, jg):
-            c = slice(512 * jg, 512 * jg + 512)
-            if jg == 0:
-                st["y", i] = work.tile([P, T], F32, tag="y", name="y")
-            y = st["y", i]
-            nc.vector.scalar_tensor_tensor(out=y[:, c], in0=st["sb", i, jg][:], scalar=st["ra", i][:], in1=st["rx", jg][:], op0=ALU.mult, op1=ALU.mult)
-            nc.sync.dma_start(out=out_0[P * i : P * i + P, c], in_=y[:, c])
-
-        def cast(i, jg):
-            c = slice(512 * jg, 512 * jg + 512)
-            if jg == 0:
-                st["yb", i] = work.tile([P, T], BF16, align_bytes=64, tag="yb", name="yb")
-            y, yb = st["y", i], st["yb", i]
-            if i < CAST_V:
-                nc.gpsimd.tensor_scalar(out=yb[:, c], in0=y[:, c], scalar1=1.0, scalar2=0.0, op0=ALU.mult, op1=ALU.add)
+        def norm(gi):
+            q = st["q", gi][:, 0 : QW * GROUP].rearrange("p (m c) -> p m c", c=QW)[:, :, 0]
+            rec = keep.tile([P, GROUP], F32, name="rec%d" % gi)
+            if gi == 0:
+                nc.vector.reciprocal(out=rec[:], in_=q)
             else:
-                nc.vector.tensor_copy(out=yb[:, c], in_=y[:, c])
+                den = work.tile([P, GROUP], F32, tag="den", name="den")
+                nc.vector.tensor_scalar(out=den[:], in0=q, scalar1=1.0 / K_CONST, scalar2=1.0, op0=ALU.mult, op1=ALU.add)
+                nc.vector.reciprocal(out=rec[:], in_=den[:])
+            st["rec", gi] = rec
 
-        words_out = out_1.bitcast(I32).rearrange("g p m o -> p g (m o)")
-        scales_out = out_2.bitcast(I32)
+        def spread(gi):
+            rx = bank("rx")
+            for k in range(GROUP):
+                nc.tensor.transpose(rx[:, P * k : P * k + P], st["rec", gi][:, k : k + 1].to_broadcast([P, P]), ident[:])
+            st["rx", gi] = rx
 
-        def tout(i, jg):
-            words = st["yb", i][:].bitcast(F32)
-            if jg == 0:
-                st["to", i] = tps.tile([P, 4, P], F32, tag="tp", name="to")
-            for u in range(2):
-                nc.tensor.transpose(st["to", i][:, 2 * jg + u, :], words[:, 256 * jg + u : 256 * (jg + 1) : 2], ident[:])
-
-        def pcopy(i, jg):
-            if jg == 0:
-                st["pg", i] = work.tile([P, 2, P, 4], BF16, align_bytes=64, tag="pg", name="pg")
-            nc.scalar.copy(out=st["pg", i][:, jg, :, :].bitcast(F32), in_=st["to", i][:, 2 * jg : 2 * jg + 2, :].rearrange("p u r -> p r u"))
-
-        def pquant(i, jg):
-            if jg == 0:
-                st["pc", i] = work.tile([P, 2, P], U32, align_bytes=64, tag="pc", name="pc")
-            pc = st["pc", i]
-            nc.vector.quantize_mx(
-                out=pc[:, jg, :].bitcast(FP8X4),
-                scales=psc[:, jg, P * i : P * i + P],
-                in_=st["pg", i][:, jg, :, :].rearrange("p r e -> p (r e)"),
+        def prod(i, gi):
+            bp = bank("bp")
+            ci, cj = slice(P * i, P * i + P), slice(512 * gi, 512 * gi + 512)
+            nc.tensor.matmul_mx(
+                out=bp[:], lhsT=c2[:, ci].bitcast(FP8X4), lhsT_scale=s2[:, ci], rhs=c2[:, cj].bitcast(FP8X4), rhs_scale=s2[:, cj], start=True, stop=True
             )
-            if jg == 1:
-                nc.sync.dma_start(out=words_out[:, :, P * i : P * i + P], in_=pc[:].bitcast(I32))
-            if i == AT - 1 and jg == 1:
+            st["bp", i] = bp
+
+        def bsq(i, gi):
+            sb = work.tile([P, 512], F32, tag="sb", name="sb")
+            nc.scalar.activation(out=sb[:], in_=st["bp", i][:], func=ACT.Square)
+            st["sb", i] = sb
+
+        def form(i, gi):
+            y = work.tile([P, 512], F32, tag="y", name="y")
+            nc.vector.scalar_tensor_tensor(
+                out=y[:], in0=st["sb", i][:], scalar=st["rec", 0][:, i : i + 1], in1=st["rx", gi][:], op0=ALU.mult, op1=ALU.mult
+            )
+            nc.sync.dma_start(out=out_0[P * i : P * i + P, 512 * (gi - 1) : 512 * gi], in_=y[:])
+            st["y", i] = y
+
+        def cast(i, gi):
+            yb = work.tile([P, 512], BF16, align_bytes=64, tag="yb", name="yb")
+            if gi == 1:
+                nc.gpsimd.tensor_scalar(out=yb[:], in0=st["y", i][:], scalar1=1.0, scalar2=0.0, op0=ALU.mult, op1=ALU.add)
+            else:
+                nc.vector.tensor_copy(out=yb[:], in_=st["y", i][:])
+            st["yb", i] = yb
+
+        def tout(i, gi):
+            words = st["yb", i][:].bitcast(F32)
+            to = bank("to")
+            for u in range(2):
+                nc.tensor.transpose(to[:, P * u : P * u + P], words[:, u:256:2], ident[:])
+            st["to", i] = to
+
+        def pcopy(i, gi):
+            pg = work.tile([P, P, 4], BF16, align_bytes=64, tag="pg", name="pg")
+            nc.scalar.copy(out=pg[:].bitcast(F32), in_=st["to", i][:, 0 : 2 * P].rearrange("p (u r) -> p r u", u=2))
+            st["pg", i] = pg
+
+        def pquant(i, gi):
+            pc = work.tile([P, P], U32, align_bytes=64, tag="pc", name="pc")
+            nc.vector.quantize_mx(out=pc[:].bitcast(FP8X4), scales=psc[:, gi - 1, P * i : P * i + P], in_=st["pg", i][:].rearrange("p r e -> p (r e)"))
+            nc.sync.dma_start(out=words_out[:, gi - 1, P * i : P * i + P], in_=pc[:].bitcast(I32))
+            if i == GROUP - 1 and gi == 2:
                 for qd in range(4):
                     nc.sync.dma_start(
                         out=scales_out[:, 4 * qd : 4 * qd + 4, :].rearrange("g q n -> q g n"),
                         in_=psc[32 * qd : 32 * qd + 4, :, :].bitcast(I32),
                     )
 
-        plan = [
-            (prod, 3, 0), (bsq, 3, 0), (prod, 3, 1), (bsq, 3, 1),
-            (tin, 0, None), (copy, 0, None), (quant2, 2, None), (s1, 1, None), (square, 1, None), (qsum, 2, None), (quant, 0, None),
-            (norm, 2, None), (inter, 1, None), (spread, 3, None),
-            (form, 3, 0), (form, 3, 1), (cast, 3, 0), (cast, 3, 1),
-            (tout, 5, 0), (tout, 5, 1), (pcopy, 5, 0), (pcopy, 5, 1), (pquant, 5, 0), (pquant, 5, 1),
-        ]
         ctx.enter_context(tc.manual_schedule())
-        for s in range(NT + 12):
-            for fn, lag, half in plan:
-                n = s - lag
-                if half is None and 0 <= n < NT:
-                    fn(n)
-                if half is not None and XT <= n < NT:
-                    fn(n - XT, half)
-            if s == 0:
+        for n in range(4):
+            tin(n)
+            copy(n)
+            quant(n)
+            if n == 0:
                 lprep()
-            if s == 1:
-                wprep()
+        wprep()
+
+        def first(gi):
+            for n in range(4 * gi, 4 * gi + 4):
+                s1(n)
+                square(n)
+                inter(n)
+                if n > 4 * gi:
+                    quant2(n - 1)
+
+        def load(gi):
+            for n in range(4 * gi, 4 * gi + 4):
+                tin(n)
+                copy(n)
+                quant(n)
+                if n == 4 * gi:
+                    quant2(n - 1)
+
+        first(0)
+        load(1)
+        for n in range(4):
+            qsum(n)
+        norm(0)
+        first(1)
+        load(2)
+        for n in range(4, 8):
+            qsum(n)
+        norm(1)
+        spread(1)
+        for i in range(4):
+            prod(i, 1)
+        for n in range(8, 12):
+            s1(n)
+        for i in range(4):
+            bsq(i, 1)
+            square(8 + i)
+            form(i, 1)
+            cast(i, 1)
+            inter(8 + i)
+            if i > 0:
+                quant2(8 + i - 1)
+        quant2(11)
+        for n in range(8, 12):
+            qsum(n)
+        for i in range(4):
+            tout(i, 1)
+            pcopy(i, 1)
+        norm(2)
+        spread(2)
+        for i in range(4):
+            prod(i, 2)
+            bsq(i, 2)
+        for i in range(4):
+            form(i, 2)
+            cast(i, 2)
+            pquant(i, 1)
+        for i in range(4):
+            tout(i, 2)
+            pcopy(i, 2)
+            pquant(i, 2)

@@ -5,9 +5,48 @@ from concourse.masks import make_identity
 
 N, T, M, R = 512, 1024, 1024, 512
 K_CONST = 1024.0
+WEIGH_V = (3, 4, 5)
+CAST_V = ((0, 1), (2, 1), (3, 2))
 P = 128
 GROUP = 4
-QW = 64
+PAIRED = ()
+TB, SB = 3, 3
+PLAN = [
+    ("cast", 1, 33),
+    ("norm", 1, 18),
+    ("tin", 0, 0),
+    ("norm", 2, 28),
+    ("recip", 2, 31),
+    ("spread", 1, 24),
+    ("copy", 0, 1),
+    ("square", 0, 3),
+    ("wprep", 0, 3),
+    ("bsq", 1, 30),
+    ("lprep", 0, 0),
+    ("quant", 0, 2),
+    ("recip", 0, 18),
+    ("quant2", 0, 8),
+    ("form", 1, 31),
+    ("tout", 2, 39),
+    ("cast", 2, 38),
+    ("tout", 1, 33),
+    ("pquant", 1, 37),
+    ("norm", 0, 14),
+    ("qsum", 0, 10),
+    ("recip", 1, 18),
+    ("pcopy", 1, 36),
+    ("form", 2, 36),
+    ("inter", 0, 4),
+    ("s1", 0, 2),
+    ("wtake", 0, 3),
+    ("weigh", 0, 4),
+    ("pquant", 2, 40),
+    ("prod", 1, 22),
+    ("bsq", 2, 34),
+    ("spread", 2, 33),
+    ("prod", 2, 28),
+    ("pcopy", 2, 39),
+]
 FLOPS = 2 * (N + T) * M * R + 2 * N * T * R
 
 F32 = mybir.dt.float32
@@ -28,10 +67,9 @@ def tile_reducedrankkellyglrtmap_kernel(tc, a, x, l_words, l_scales, w, out_0, o
         keep = ctx.enter_context(tc.tile_pool(name="keep", bufs=1))
         raw = ctx.enter_context(tc.tile_pool(name="raw", bufs=NT))
         work = ctx.enter_context(tc.tile_pool(name="work", bufs=5))
-        psum = ctx.enter_context(tc.psum_pool(name="psum", bufs=8))
-
-        def bank(name):
-            return psum.tile([P, 512], F32, tag="bank", name=name)
+        turns = ctx.enter_context(tc.psum_pool(name="turns", bufs=TB))
+        sums = ctx.enter_context(tc.psum_pool(name="sums", bufs=SB))
+        norms = ctx.enter_context(tc.psum_pool(name="norms", bufs=2))
 
         scr = keep.tile([P, 2, 512], U8, align_bytes=64, name="scr")
         nc.vector.memset(scr[:].rearrange("p g n -> p (g n)").bitcast(I32), 0)
@@ -64,14 +102,14 @@ def tile_reducedrankkellyglrtmap_kernel(tc, a, x, l_words, l_scales, w, out_0, o
                     out=wt[0:4, :].rearrange("t (b i) -> t b i", i=8),
                     in_=w.rearrange("(b t i) -> t b i", t=4, i=8),
                 )
-            if n == 1:
+            if n == 0:
                 nc.sync.dma_start(out=lw[:].bitcast(I32), in_=l_words.bitcast(I32).rearrange("g p n -> p g n"))
 
         lp = keep.tile([P, 2, 4, 256], U8, align_bytes=64, name="lp")
         sp = keep.tile([P, 2, 4, P], U8, align_bytes=64, name="sp")
         wf = keep.tile([P, P], F32, name="wf")
         wcol = keep.tile([P, 4], F32, name="wcol")
-        wrep = keep.tile([P, 4, QW], F32, name="wrep")
+        wcolk = keep.tile([P, 4], F32, name="wcolk")
 
         def lprep():
             for g in range(2):
@@ -87,10 +125,13 @@ def tile_reducedrankkellyglrtmap_kernel(tc, a, x, l_words, l_scales, w, out_0, o
 
         def wprep():
             nc.vector.tensor_copy(out=wf[:], in_=wt[:])
-            wps = bank("wps")
+            wps = turns.tile([P, 512], F32, tag="turn", name="wps")
             nc.tensor.transpose(wps[:, 0:P], wf[:], ident[:])
-            nc.vector.tensor_copy(out=wcol[:], in_=wps[:, 0:4])
-            nc.vector.tensor_copy(out=wrep[:], in_=wcol[:].unsqueeze(2).to_broadcast([P, 4, QW]))
+            st["wps"] = wps
+
+        def wtake():
+            nc.vector.tensor_copy(out=wcol[:], in_=st["wps"][:, 0:4])
+            nc.vector.tensor_scalar(out=wcolk[:], in0=st["wps"][:, 0:4], scalar1=1.0 / K_CONST, scalar2=0.0, op0=ALU.mult, op1=ALU.add)
 
         c2 = keep.tile([P, N + T], U32, align_bytes=64, name="c2")
         s2 = keep.tile([P, N + T], U8, align_bytes=64, name="s2")
@@ -101,7 +142,7 @@ def tile_reducedrankkellyglrtmap_kernel(tc, a, x, l_words, l_scales, w, out_0, o
 
         def tin(n):
             words = tiles[n][:].bitcast(F32)
-            tp = bank("tp")
+            tp = turns.tile([P, 512], F32, tag="turn", name="tp")
             for g in range(2):
                 for u in range(2):
                     k = 2 * g + u
@@ -121,7 +162,7 @@ def tile_reducedrankkellyglrtmap_kernel(tc, a, x, l_words, l_scales, w, out_0, o
             st["xs", n] = xs
 
         def s1(n):
-            ps = bank("ps")
+            ps = sums.tile([P, 512], F32, tag="sum", name="ps")
             for t in range(4):
                 for g in range(2):
                     c = slice(P * g, P * g + P)
@@ -137,9 +178,19 @@ def tile_reducedrankkellyglrtmap_kernel(tc, a, x, l_words, l_scales, w, out_0, o
             st["ps", n] = ps
 
         def square(n):
-            sq = work.tile([P, 4, P], F32, tag="sq", name="sq")
-            nc.scalar.activation(out=sq[:], in_=st["ps", n][:].rearrange("p (t n) -> p t n", t=4), func=ACT.Square)
-            st["sq", n] = sq
+            if n % 2 == 0:
+                st["sq", n // 2] = work.tile([P, 4, 2, P], F32, tag="sq", name="sq")
+            nc.scalar.activation(
+                out=st["sq", n // 2][:, :, n % 2, :], in_=st["ps", n][:].rearrange("p (t n) -> p t n", t=4), func=ACT.Square
+            )
+
+        def weigh(h):
+            sq = st["sq", h]
+            eng = nc.vector if h in WEIGH_V else nc.gpsimd
+            col = wcolk if 2 * h < GROUP else wcol
+            for t in range(4):
+                extra = K_CONST / P if 2 * h >= GROUP and t == 0 else 0.0
+                eng.tensor_scalar(out=sq[:, t, :, :], in0=sq[:, t, :, :], scalar1=col[:, t : t + 1], scalar2=extra, op0=ALU.mult, op1=ALU.add)
 
         def inter(n):
             xb = work.tile([P, P, 4], BF16, align_bytes=64, tag="xb", name="xb")
@@ -157,72 +208,73 @@ def tile_reducedrankkellyglrtmap_kernel(tc, a, x, l_words, l_scales, w, out_0, o
         def qsum(n):
             gi, m = divmod(n, GROUP)
             if m == 0:
-                st["q", gi] = bank("qs")
+                st["q", gi] = norms.tile([P, 512], F32, tag="norm", name="qs")
             q = st["q", gi]
             for t in range(4):
-                nc.tensor.matmul(q[:, QW * m : QW * m + QW], st["sq", n][:, t, :], wrep[:, t, :], start=(t == 0), stop=(t == 3))
+                nc.tensor.matmul(
+                    q[:, P * m : P * m + P], st["sq", n // 2][:, t, n % 2, :], ident[:], start=(t == 0), stop=(t == 3), is_transpose=True
+                )
 
         def norm(gi):
-            q = st["q", gi][:, 0 : QW * GROUP].rearrange("p (m c) -> p m c", c=QW)[:, :, 0]
+            qf = work.tile([P, GROUP], F32, tag="qf", name="qf")
+            nc.vector.tensor_reduce(out=qf[:], in_=st["q", gi][:].rearrange("p (m r) -> p m r", m=GROUP), axis=mybir.AxisListType.X, op=ALU.add)
+            st["qf", gi] = qf
+
+        def recip(gi):
             rec = keep.tile([P, GROUP], F32, name="rec%d" % gi)
-            if gi == 0:
-                nc.vector.reciprocal(out=rec[:], in_=q)
-            else:
-                den = work.tile([P, GROUP], F32, tag="den", name="den")
-                nc.vector.tensor_scalar(out=den[:], in0=q, scalar1=1.0 / K_CONST, scalar2=1.0, op0=ALU.mult, op1=ALU.add)
-                nc.vector.reciprocal(out=rec[:], in_=den[:])
+            nc.vector.reciprocal(out=rec[:], in_=st["qf", gi][:])
             st["rec", gi] = rec
 
         def spread(gi):
-            rx = bank("rx")
+            rx = norms.tile([P, 512], F32, tag="norm", name="rx")
             for k in range(GROUP):
                 nc.tensor.transpose(rx[:, P * k : P * k + P], st["rec", gi][:, k : k + 1].to_broadcast([P, P]), ident[:])
             st["rx", gi] = rx
 
         def prod(i, gi):
-            bp = bank("bp")
+            bp = sums.tile([P, 512], F32, tag="sum", name="bp")
             ci, cj = slice(P * i, P * i + P), slice(512 * gi, 512 * gi + 512)
             nc.tensor.matmul_mx(
                 out=bp[:], lhsT=c2[:, ci].bitcast(FP8X4), lhsT_scale=s2[:, ci], rhs=c2[:, cj].bitcast(FP8X4), rhs_scale=s2[:, cj], start=True, stop=True
             )
-            st["bp", i] = bp
+            st["bp", i, gi] = bp
 
         def bsq(i, gi):
             sb = work.tile([P, 512], F32, tag="sb", name="sb")
-            nc.scalar.activation(out=sb[:], in_=st["bp", i][:], func=ACT.Square)
-            st["sb", i] = sb
+            nc.scalar.activation(out=sb[:], in_=st["bp", i, gi][:], func=ACT.Square)
+            st["sb", i, gi] = sb
 
         def form(i, gi):
             y = work.tile([P, 512], F32, tag="y", name="y")
             nc.vector.scalar_tensor_tensor(
-                out=y[:], in0=st["sb", i][:], scalar=st["rec", 0][:, i : i + 1], in1=st["rx", gi][:], op0=ALU.mult, op1=ALU.mult
+                out=y[:], in0=st["sb", i, gi][:], scalar=st["rec", 0][:, i : i + 1], in1=st["rx", gi][:], op0=ALU.mult, op1=ALU.mult
             )
             nc.sync.dma_start(out=out_0[P * i : P * i + P, 512 * (gi - 1) : 512 * gi], in_=y[:])
-            st["y", i] = y
+            st["y", i, gi] = y
 
         def cast(i, gi):
             yb = work.tile([P, 512], BF16, align_bytes=64, tag="yb", name="yb")
-            if gi == 1:
-                nc.gpsimd.tensor_scalar(out=yb[:], in0=st["y", i][:], scalar1=1.0, scalar2=0.0, op0=ALU.mult, op1=ALU.add)
+            if (i, gi) not in CAST_V:
+                nc.gpsimd.tensor_scalar(out=yb[:], in0=st["y", i, gi][:], scalar1=1.0, scalar2=0.0, op0=ALU.mult, op1=ALU.add)
             else:
-                nc.vector.tensor_copy(out=yb[:], in_=st["y", i][:])
-            st["yb", i] = yb
+                nc.vector.tensor_copy(out=yb[:], in_=st["y", i, gi][:])
+            st["yb", i, gi] = yb
 
         def tout(i, gi):
-            words = st["yb", i][:].bitcast(F32)
-            to = bank("to")
+            words = st["yb", i, gi][:].bitcast(F32)
+            to = turns.tile([P, 512], F32, tag="turn", name="to")
             for u in range(2):
                 nc.tensor.transpose(to[:, P * u : P * u + P], words[:, u:256:2], ident[:])
-            st["to", i] = to
+            st["to", i, gi] = to
 
         def pcopy(i, gi):
             pg = work.tile([P, P, 4], BF16, align_bytes=64, tag="pg", name="pg")
-            nc.scalar.copy(out=pg[:].bitcast(F32), in_=st["to", i][:, 0 : 2 * P].rearrange("p (u r) -> p r u", u=2))
-            st["pg", i] = pg
+            nc.scalar.copy(out=pg[:].bitcast(F32), in_=st["to", i, gi][:, 0 : 2 * P].rearrange("p (u r) -> p r u", u=2))
+            st["pg", i, gi] = pg
 
         def pquant(i, gi):
             pc = work.tile([P, P], U32, align_bytes=64, tag="pc", name="pc")
-            nc.vector.quantize_mx(out=pc[:].bitcast(FP8X4), scales=psc[:, gi - 1, P * i : P * i + P], in_=st["pg", i][:].rearrange("p r e -> p (r e)"))
+            nc.vector.quantize_mx(out=pc[:].bitcast(FP8X4), scales=psc[:, gi - 1, P * i : P * i + P], in_=st["pg", i, gi][:].rearrange("p r e -> p (r e)"))
             nc.sync.dma_start(out=words_out[:, gi - 1, P * i : P * i + P], in_=pc[:].bitcast(I32))
             if i == GROUP - 1 and gi == 2:
                 for qd in range(4):
@@ -232,69 +284,26 @@ def tile_reducedrankkellyglrtmap_kernel(tc, a, x, l_words, l_scales, w, out_0, o
                     )
 
         ctx.enter_context(tc.manual_schedule())
-        for n in range(4):
-            tin(n)
-            copy(n)
-            quant(n)
-            if n == 0:
-                lprep()
-        wprep()
-
-        def first(gi):
-            for n in range(4 * gi, 4 * gi + 4):
-                s1(n)
-                square(n)
-                inter(n)
-                if n > 4 * gi:
-                    quant2(n - 1)
-
-        def load(gi):
-            for n in range(4 * gi, 4 * gi + 4):
-                tin(n)
-                copy(n)
-                quant(n)
-                if n == 4 * gi:
-                    quant2(n - 1)
-
-        first(0)
-        load(1)
-        for n in range(4):
-            qsum(n)
-        norm(0)
-        first(1)
-        load(2)
-        for n in range(4, 8):
-            qsum(n)
-        norm(1)
-        spread(1)
-        for i in range(4):
-            prod(i, 1)
-        for n in range(8, 12):
-            s1(n)
-        for i in range(4):
-            bsq(i, 1)
-            square(8 + i)
-            form(i, 1)
-            cast(i, 1)
-            inter(8 + i)
-            if i > 0:
-                quant2(8 + i - 1)
-        quant2(11)
-        for n in range(8, 12):
-            qsum(n)
-        for i in range(4):
-            tout(i, 1)
-            pcopy(i, 1)
-        norm(2)
-        spread(2)
-        for i in range(4):
-            prod(i, 2)
-            bsq(i, 2)
-        for i in range(4):
-            form(i, 2)
-            cast(i, 2)
-            pquant(i, 1)
-        for i in range(4):
-            tout(i, 2)
-            pcopy(i, 2)
-            pquant(i, 2)
+        FN = dict(lprep=lprep, wprep=wprep, wtake=wtake, tin=tin, copy=copy, quant=quant, s1=s1, square=square, inter=inter, quant2=quant2, weigh=weigh, qsum=qsum, norm=norm, recip=recip, spread=spread, prod=prod, bsq=bsq, form=form, cast=cast, tout=tout, pcopy=pcopy, pquant=pquant)
+        for s in range(44):
+            for name, gi, lag in PLAN:
+                fn = FN[name]
+                n = s - lag
+                if name in ("tin", "copy", "quant", "s1", "square", "inter", "quant2", "qsum"):
+                    if name in PAIRED:
+                        if 0 <= n < NT and n % 2 == 0:
+                            fn(n)
+                            fn(n + 1)
+                    elif 0 <= n < NT:
+                        fn(n)
+                elif name == "weigh":
+                    if 0 <= n < NT and n % 2 == 1:
+                        fn(n // 2)
+                elif name in ("norm", "recip", "spread"):
+                    if n == 0:
+                        fn(gi)
+                elif name in ("lprep", "wprep", "wtake"):
+                    if n == 0:
+                        fn()
+                elif 0 <= n < GROUP:
+                    fn(n, gi)

@@ -5,47 +5,49 @@ from concourse.masks import make_identity
 
 N, T, M, R = 512, 1024, 1024, 512
 K_CONST = 1024.0
-WEIGH_V = (3, 4, 5)
-CAST_V = ((0, 1), (2, 1), (3, 2))
+WEIGH_V = (0, 3, 4)
+CAST_V = ((1, 2), (3, 1), (3, 2))
 P = 128
 GROUP = 4
-PAIRED = ()
+PAIRED = ("tin", "s1", "qsum")
+INTER_S = (4, 5, 8, 11)
+RED_S = (0,)
 TB, SB = 3, 3
 PLAN = [
-    ("cast", 1, 33),
-    ("norm", 1, 18),
     ("tin", 0, 0),
-    ("norm", 2, 28),
-    ("recip", 2, 31),
-    ("spread", 1, 24),
-    ("copy", 0, 1),
+    ("quant", 0, 1),
+    ("tout", 1, 32),
+    ("pquant", 1, 35),
     ("square", 0, 3),
-    ("wprep", 0, 3),
-    ("bsq", 1, 30),
-    ("lprep", 0, 0),
-    ("quant", 0, 2),
-    ("recip", 0, 18),
-    ("quant2", 0, 8),
-    ("form", 1, 31),
-    ("tout", 2, 39),
-    ("cast", 2, 38),
-    ("tout", 1, 33),
-    ("pquant", 1, 37),
-    ("norm", 0, 14),
-    ("qsum", 0, 10),
-    ("recip", 1, 18),
-    ("pcopy", 1, 36),
-    ("form", 2, 36),
-    ("inter", 0, 4),
-    ("s1", 0, 2),
-    ("wtake", 0, 3),
+    ("spread", 1, 19),
+    ("bsq", 2, 30),
+    ("inter", 0, 3),
+    ("tout", 2, 36),
     ("weigh", 0, 4),
-    ("pquant", 2, 40),
-    ("prod", 1, 22),
-    ("bsq", 2, 34),
-    ("spread", 2, 33),
+    ("form", 2, 32),
+    ("prod", 1, 17),
+    ("lprep", 0, 1),
     ("prod", 2, 28),
-    ("pcopy", 2, 39),
+    ("bsq", 1, 17),
+    ("recip", 2, 25),
+    ("spread", 2, 30),
+    ("copy", 0, 0),
+    ("s1", 0, 2),
+    ("qsum", 0, 10),
+    ("pquant", 2, 38),
+    ("norm", 1, 17),
+    ("form", 1, 22),
+    ("pcopy", 1, 33),
+    ("recip", 1, 18),
+    ("cast", 1, 28),
+    ("wprep", 0, 2),
+    ("recip", 0, 21),
+    ("norm", 2, 24),
+    ("quant2", 0, 6),
+    ("norm", 0, 15),
+    ("pcopy", 2, 36),
+    ("wtake", 0, 2),
+    ("cast", 2, 34),
 ]
 FLOPS = 2 * (N + T) * M * R + 2 * N * T * R
 
@@ -86,13 +88,10 @@ def tile_reducedrankkellyglrtmap_kernel(tc, a, x, l_words, l_scales, w, out_0, o
         tiles = []
         for n in range(NT):
             rt = raw.tile([P, M], BF16, align_bytes=64, name="rt")
-            if n == 0:
-                for h in range(2):
-                    nc.sync.dma_start(out=rt[:, 512 * h : 512 * h + 512], in_=rows[n][:, 512 * h : 512 * h + 512])
-            else:
-                nc.sync.dma_start(out=rt[:], in_=rows[n])
+            nc.sync.dma_start(out=rt[:], in_=rows[n])
             tiles.append(rt)
-            if n == 0:
+            if n == GROUP - 1:
+                nc.sync.dma_start(out=lw[:].bitcast(I32), in_=l_words.bitcast(I32).rearrange("g p n -> p g n"))
                 for qd in range(4):
                     nc.scalar.dma_start(
                         out=scr[32 * qd : 32 * qd + 4, :, :].bitcast(I32),
@@ -102,8 +101,6 @@ def tile_reducedrankkellyglrtmap_kernel(tc, a, x, l_words, l_scales, w, out_0, o
                     out=wt[0:4, :].rearrange("t (b i) -> t b i", i=8),
                     in_=w.rearrange("(b t i) -> t b i", t=4, i=8),
                 )
-            if n == 0:
-                nc.sync.dma_start(out=lw[:].bitcast(I32), in_=l_words.bitcast(I32).rearrange("g p n -> p g n"))
 
         lp = keep.tile([P, 2, 4, 256], U8, align_bytes=64, name="lp")
         sp = keep.tile([P, 2, 4, P], U8, align_bytes=64, name="sp")
@@ -195,7 +192,9 @@ def tile_reducedrankkellyglrtmap_kernel(tc, a, x, l_words, l_scales, w, out_0, o
         def inter(n):
             xb = work.tile([P, P, 4], BF16, align_bytes=64, tag="xb", name="xb")
             src = st["ps", n][:].rearrange("p (t n) -> p n t", t=4)
-            if n >= GROUP:
+            if n in INTER_S:
+                nc.scalar.copy(out=xb[:], in_=src)
+            elif n >= GROUP:
                 nc.vector.tensor_copy(out=xb[:], in_=src)
             else:
                 nc.vector.tensor_tensor(out=xb[:], in0=src, in1=wcol[:].unsqueeze(1).to_broadcast([P, P, 4]), op=ALU.mult)
@@ -217,7 +216,12 @@ def tile_reducedrankkellyglrtmap_kernel(tc, a, x, l_words, l_scales, w, out_0, o
 
         def norm(gi):
             qf = work.tile([P, GROUP], F32, tag="qf", name="qf")
-            nc.vector.tensor_reduce(out=qf[:], in_=st["q", gi][:].rearrange("p (m r) -> p m r", m=GROUP), axis=mybir.AxisListType.X, op=ALU.add)
+            if gi in RED_S:
+                for m in range(GROUP):
+                    junk = work.tile([P, P], F32, tag="junk", name="junk")
+                    nc.scalar.activation(out=junk[:], in_=st["q", gi][:, P * m : P * m + P], func=ACT.Copy, accum_out=qf[:, m : m + 1])
+            else:
+                nc.vector.tensor_reduce(out=qf[:], in_=st["q", gi][:].rearrange("p (m r) -> p m r", m=GROUP), axis=mybir.AxisListType.X, op=ALU.add)
             st["qf", gi] = qf
 
         def recip(gi):

from contextlib import ExitStack

import concourse.mybir as mybir
from concourse.masks import make_identity

N, T, M, R = 512, 1024, 1024, 512
K_CONST = 1024.0
WEIGH_V = (0, 3, 4)
CAST_V = ((1, 2), (3, 1), (3, 2))
P = 128
GROUP = 4
PAIRED = ("tin", "s1", "qsum")
INTER_S = (4, 5, 8, 11)
RED_S = (0,)
TB, SB = 3, 3
PLAN = [
    ("tin", 0, 0),
    ("quant", 0, 1),
    ("tout", 1, 32),
    ("pquant", 1, 35),
    ("square", 0, 3),
    ("spread", 1, 19),
    ("bsq", 2, 30),
    ("inter", 0, 3),
    ("tout", 2, 36),
    ("weigh", 0, 4),
    ("form", 2, 32),
    ("prod", 1, 17),
    ("lprep", 0, 1),
    ("prod", 2, 28),
    ("bsq", 1, 17),
    ("recip", 2, 25),
    ("spread", 2, 30),
    ("copy", 0, 0),
    ("s1", 0, 2),
    ("qsum", 0, 10),
    ("pquant", 2, 38),
    ("norm", 1, 17),
    ("form", 1, 22),
    ("pcopy", 1, 33),
    ("recip", 1, 18),
    ("cast", 1, 28),
    ("wprep", 0, 2),
    ("recip", 0, 21),
    ("norm", 2, 24),
    ("quant2", 0, 6),
    ("norm", 0, 15),
    ("pcopy", 2, 36),
    ("wtake", 0, 2),
    ("cast", 2, 34),
]
FLOPS = 2 * (N + T) * M * R + 2 * N * T * R

F32 = mybir.dt.float32
BF16 = mybir.dt.bfloat16
U32 = mybir.dt.uint32
I32 = mybir.dt.int32
U8 = mybir.dt.uint8
FP8X4 = mybir.dt.float8_e4m3fn_x4
FP4X4 = mybir.dt.float4_e2m1fn_x4
ALU = mybir.AluOpType
ACT = mybir.ActivationFunctionType


def tile_reducedrankkellyglrtmap_kernel(tc, a, x, l_words, l_scales, w, out_0, out_1, out_2):
    nc = tc.nc
    NT = (N + T) // P
    with ExitStack() as ctx:
        keep = ctx.enter_context(tc.tile_pool(name="keep", bufs=1))
        raw = ctx.enter_context(tc.tile_pool(name="raw", bufs=NT))
        work = ctx.enter_context(tc.tile_pool(name="work", bufs=5))
        turns = ctx.enter_context(tc.psum_pool(name="turns", bufs=TB))
        sums = ctx.enter_context(tc.psum_pool(name="sums", bufs=SB))
        norms = ctx.enter_context(tc.psum_pool(name="norms", bufs=2))

        scr = keep.tile([P, 2, 512], U8, align_bytes=64, name="scr")
        nc.vector.memset(scr[:].rearrange("p g n -> p (g n)").bitcast(I32), 0)
        wt = keep.tile([P, P], BF16, align_bytes=64, name="wt")
        nc.vector.memset(wt[:], 0.0)
        warm = keep.tile([P, 4], F32, name="warm")
        nc.vector.memset(warm[:], 0.0)
        nc.scalar.activation(out=warm[:], in_=warm[:], func=ACT.Square)
        ident = keep.tile([P, P], F32, align_bytes=64, name="ident")
        make_identity(nc, ident[:])

        rows = [a[P * i : P * i + P, :] for i in range(N // P)] + [x[P * i : P * i + P, :] for i in range(T // P)]
        lw = keep.tile([P, 2, 1024], U8, align_bytes=64, name="lw")
        tiles = []
        for n in range(NT):
            rt = raw.tile([P, M], BF16, align_bytes=64, name="rt")
            nc.sync.dma_start(out=rt[:], in_=rows[n])
            tiles.append(rt)
            if n == GROUP - 1:
                nc.sync.dma_start(out=lw[:].bitcast(I32), in_=l_words.bitcast(I32).rearrange("g p n -> p g n"))
                for qd in range(4):
                    nc.scalar.dma_start(
                        out=scr[32 * qd : 32 * qd + 4, :, :].bitcast(I32),
                        in_=l_scales[:, 4 * qd : 4 * qd + 4, :].bitcast(I32).rearrange("g q n -> q g n"),
                    )
                nc.scalar.dma_start(
                    out=wt[0:4, :].rearrange("t (b i) -> t b i", i=8),
                    in_=w.rearrange("(b t i) -> t b i", t=4, i=8),
                )

        lp = keep.tile([P, 2, 4, 256], U8, align_bytes=64, name="lp")
        sp = keep.tile([P, 2, 4, P], U8, align_bytes=64, name="sp")
        wf = keep.tile([P, P], F32, name="wf")
        wcol = keep.tile([P, 4], F32, name="wcol")
        wcolk = keep.tile([P, 4], F32, name="wcolk")

        def lprep():
            for g in range(2):
                nc.vector.tensor_copy(
                    out=lp[:, g, :, :].bitcast(I32).rearrange("p t (b i) -> p t b i", i=4),
                    in_=lw[:, g, :].bitcast(I32).rearrange("p (b t i) -> p t b i", t=4, i=4),
                )
            for g in range(2):
                nc.vector.tensor_copy(
                    out=sp[:, g, :, :].bitcast(I32).rearrange("p t (b i) -> p t b i", i=2),
                    in_=scr[:, g, :].bitcast(I32).rearrange("p (b t i) -> p t b i", t=4, i=2),
                )

        def wprep():
            nc.vector.tensor_copy(out=wf[:], in_=wt[:])
            wps = turns.tile([P, 512], F32, tag="turn", name="wps")
            nc.tensor.transpose(wps[:, 0:P], wf[:], ident[:])
            st["wps"] = wps

        def wtake():
            nc.vector.tensor_copy(out=wcol[:], in_=st["wps"][:, 0:4])
            nc.vector.tensor_scalar(out=wcolk[:], in0=st["wps"][:, 0:4], scalar1=1.0 / K_CONST, scalar2=0.0, op0=ALU.mult, op1=ALU.add)

        c2 = keep.tile([P, N + T], U32, align_bytes=64, name="c2")
        s2 = keep.tile([P, N + T], U8, align_bytes=64, name="s2")
        psc = keep.tile([P, 2, N], U8, align_bytes=64, name="psc")
        words_out = out_1.bitcast(I32).rearrange("g p m o -> p g (m o)")
        scales_out = out_2.bitcast(I32)
        st = {}

        def tin(n):
            words = tiles[n][:].bitcast(F32)
            tp = turns.tile([P, 512], F32, tag="turn", name="tp")
            for g in range(2):
                for u in range(2):
                    k = 2 * g + u
                    nc.tensor.transpose(tp[:, P * k : P * k + P], words[:, 256 * g + u : 256 * (g + 1) : 2], ident[:])
            st["tp", n] = tp

        def copy(n):
            xg = work.tile([P, 2, P, 4], BF16, align_bytes=64, tag="xg", name="xg")
            nc.scalar.copy(out=xg[:].bitcast(F32), in_=st["tp", n][:].rearrange("p (g u r) -> p g r u", g=2, u=2))
            st["xg", n] = xg

        def quant(n):
            xc = work.tile([P, 2 * P], U32, align_bytes=64, tag="xc", name="xc")
            xs = work.tile([P, 2 * P], U8, align_bytes=64, tag="xs", name="xs")
            nc.vector.quantize_mx(out=xc[:].bitcast(FP8X4), scales=xs[:], in_=st["xg", n][:].rearrange("p g r e -> p (g r e)"))
            st["xc", n] = xc
            st["xs", n] = xs

        def s1(n):
            ps = sums.tile([P, 512], F32, tag="sum", name="ps")
            for t in range(4):
                for g in range(2):
                    c = slice(P * g, P * g + P)
                    nc.tensor.matmul_mx(
                        out=ps[:, P * t : P * t + P],
                        lhsT=lp[:, g, t, :].bitcast(FP4X4),
                        lhsT_scale=sp[:, g, t, :],
                        rhs=st["xc", n][:, c].bitcast(FP8X4),
                        rhs_scale=st["xs", n][:, c],
                        start=(g == 0),
                        stop=(g == 1),
                    )
            st["ps", n] = ps

        def square(n):
            if n % 2 == 0:
                st["sq", n // 2] = work.tile([P, 4, 2, P], F32, tag="sq", name="sq")
            nc.scalar.activation(
                out=st["sq", n // 2][:, :, n % 2, :], in_=st["ps", n][:].rearrange("p (t n) -> p t n", t=4), func=ACT.Square
            )

        def weigh(h):
            sq = st["sq", h]
            eng = nc.vector if h in WEIGH_V else nc.gpsimd
            col = wcolk if 2 * h < GROUP else wcol
            for t in range(4):
                extra = K_CONST / P if 2 * h >= GROUP and t == 0 else 0.0
                eng.tensor_scalar(out=sq[:, t, :, :], in0=sq[:, t, :, :], scalar1=col[:, t : t + 1], scalar2=extra, op0=ALU.mult, op1=ALU.add)

        def inter(n):
            xb = work.tile([P, P, 4], BF16, align_bytes=64, tag="xb", name="xb")
            src = st["ps", n][:].rearrange("p (t n) -> p n t", t=4)
            if n in INTER_S:
                nc.scalar.copy(out=xb[:], in_=src)
            elif n >= GROUP:
                nc.vector.tensor_copy(out=xb[:], in_=src)
            else:
                nc.vector.tensor_tensor(out=xb[:], in0=src, in1=wcol[:].unsqueeze(1).to_broadcast([P, P, 4]), op=ALU.mult)
            st["xb", n] = xb

        def quant2(n):
            c = slice(P * n, P * n + P)
            nc.vector.quantize_mx(out=c2[:, c].bitcast(FP8X4), scales=s2[:, c], in_=st["xb", n][:].rearrange("p n t -> p (n t)"))

        def qsum(n):
            gi, m = divmod(n, GROUP)
            if m == 0:
                st["q", gi] = norms.tile([P, 512], F32, tag="norm", name="qs")
            q = st["q", gi]
            for t in range(4):
                nc.tensor.matmul(
                    q[:, P * m : P * m + P], st["sq", n // 2][:, t, n % 2, :], ident[:], start=(t == 0), stop=(t == 3), is_transpose=True
                )

        def norm(gi):
            qf = work.tile([P, GROUP], F32, tag="qf", name="qf")
            if gi in RED_S:
                for m in range(GROUP):
                    junk = work.tile([P, P], F32, tag="junk", name="junk")
                    nc.scalar.activation(out=junk[:], in_=st["q", gi][:, P * m : P * m + P], func=ACT.Copy, accum_out=qf[:, m : m + 1])
            else:
                nc.vector.tensor_reduce(out=qf[:], in_=st["q", gi][:].rearrange("p (m r) -> p m r", m=GROUP), axis=mybir.AxisListType.X, op=ALU.add)
            st["qf", gi] = qf

        def recip(gi):
            rec = keep.tile([P, GROUP], F32, name="rec%d" % gi)
            nc.vector.reciprocal(out=rec[:], in_=st["qf", gi][:])
            st["rec", gi] = rec

        def spread(gi):
            rx = norms.tile([P, 512], F32, tag="norm", name="rx")
            for k in range(GROUP):
                nc.tensor.transpose(rx[:, P * k : P * k + P], st["rec", gi][:, k : k + 1].to_broadcast([P, P]), ident[:])
            st["rx", gi] = rx

        def prod(i, gi):
            bp = sums.tile([P, 512], F32, tag="sum", name="bp")
            ci, cj = slice(P * i, P * i + P), slice(512 * gi, 512 * gi + 512)
            nc.tensor.matmul_mx(
                out=bp[:], lhsT=c2[:, ci].bitcast(FP8X4), lhsT_scale=s2[:, ci], rhs=c2[:, cj].bitcast(FP8X4), rhs_scale=s2[:, cj], start=True, stop=True
            )
            st["bp", i, gi] = bp

        def bsq(i, gi):
            sb = work.tile([P, 512], F32, tag="sb", name="sb")
            nc.scalar.activation(out=sb[:], in_=st["bp", i, gi][:], func=ACT.Square)
            st["sb", i, gi] = sb

        def form(i, gi):
            y = work.tile([P, 512], F32, tag="y", name="y")
            nc.vector.scalar_tensor_tensor(
                out=y[:], in0=st["sb", i, gi][:], scalar=st["rec", 0][:, i : i + 1], in1=st["rx", gi][:], op0=ALU.mult, op1=ALU.mult
            )
            nc.sync.dma_start(out=out_0[P * i : P * i + P, 512 * (gi - 1) : 512 * gi], in_=y[:])
            st["y", i, gi] = y

        def cast(i, gi):
            yb = work.tile([P, 512], BF16, align_bytes=64, tag="yb", name="yb")
            if (i, gi) not in CAST_V:
                nc.gpsimd.tensor_scalar(out=yb[:], in0=st["y", i, gi][:], scalar1=1.0, scalar2=0.0, op0=ALU.mult, op1=ALU.add)
            else:
                nc.vector.tensor_copy(out=yb[:], in_=st["y", i, gi][:])
            st["yb", i, gi] = yb

        def tout(i, gi):
            words = st["yb", i, gi][:].bitcast(F32)
            to = turns.tile([P, 512], F32, tag="turn", name="to")
            for u in range(2):
                nc.tensor.transpose(to[:, P * u : P * u + P], words[:, u:256:2], ident[:])
            st["to", i, gi] = to

        def pcopy(i, gi):
            pg = work.tile([P, P, 4], BF16, align_bytes=64, tag="pg", name="pg")
            nc.scalar.copy(out=pg[:].bitcast(F32), in_=st["to", i, gi][:, 0 : 2 * P].rearrange("p (u r) -> p r u", u=2))
            st["pg", i, gi] = pg

        def pquant(i, gi):
            pc = work.tile([P, P], U32, align_bytes=64, tag="pc", name="pc")
            nc.vector.quantize_mx(out=pc[:].bitcast(FP8X4), scales=psc[:, gi - 1, P * i : P * i + P], in_=st["pg", i, gi][:].rearrange("p r e -> p (r e)"))
            nc.sync.dma_start(out=words_out[:, gi - 1, P * i : P * i + P], in_=pc[:].bitcast(I32))
            if i == GROUP - 1 and gi == 2:
                for qd in range(4):
                    nc.sync.dma_start(
                        out=scales_out[:, 4 * qd : 4 * qd + 4, :].rearrange("g q n -> q g n"),
                        in_=psc[32 * qd : 32 * qd + 4, :, :].bitcast(I32),
                    )

        ctx.enter_context(tc.manual_schedule())
        FN = dict(lprep=lprep, wprep=wprep, wtake=wtake, tin=tin, copy=copy, quant=quant, s1=s1, square=square, inter=inter, quant2=quant2, weigh=weigh, qsum=qsum, norm=norm, recip=recip, spread=spread, prod=prod, bsq=bsq, form=form, cast=cast, tout=tout, pcopy=pcopy, pquant=pquant)
        for s in range(44):
            for name, gi, lag in PLAN:
                fn = FN[name]
                n = s - lag
                if name in ("tin", "copy", "quant", "s1", "square", "inter", "quant2", "qsum"):
                    if name in PAIRED:
                        if 0 <= n < NT and n % 2 == 0:
                            fn(n)
                            fn(n + 1)
                    elif 0 <= n < NT:
                        fn(n)
                elif name == "weigh":
                    if 0 <= n < NT and n % 2 == 1:
                        fn(n // 2)
                elif name in ("norm", "recip", "spread"):
                    if n == 0:
                        fn(gi)
                elif name in ("lprep", "wprep", "wtake"):
                    if n == 0:
                        fn()
                elif 0 <= n < GROUP:
                    fn(n, gi)
